import numpy as np
import ml_dtypes


def mxq(x, axis, fmt="e4m3"):
    dtype, down = {"e4m3": (ml_dtypes.float8_e4m3fn, 7), "e5m2": (ml_dtypes.float8_e5m2, 14)}[fmt]
    v = np.moveaxis(np.asarray(x, np.float32).astype(ml_dtypes.bfloat16).astype(np.float64), axis, -1)
    blocks = v.reshape(v.shape[:-1] + (-1, 32))
    amax = np.abs(blocks).max(-1, keepdims=True)
    byte = np.maximum(np.where(amax > 0, np.frexp(amax)[1] - 1 + 127, 0) - down, 1)
    scale = np.exp2(byte - 127.0)
    codes = (blocks / scale).astype(np.float32).astype(dtype).astype(np.float64)
    return np.moveaxis((codes * scale).reshape(v.shape), -1, axis)


WIDE = False


def mx_kscale(k):
    if not WIDE:
        return np.ones(k)
    levels = np.array([10, -10, 5, -5, 0])
    if k % 512:
        return np.exp2(np.random.permutation(np.resize(levels, k // 32))).repeat(32)
    a = np.empty((k // 512, 16))
    for p in range(k // 512):
        a[p, :8] = np.random.permutation(np.resize(levels, 8))
        for g in range(8):
            far = levels[np.abs(levels - a[p, g]) >= 10]
            a[p, g + 8] = far[np.random.randint(len(far))]
    return np.exp2(a.ravel()).repeat(32)


def f64(x):
    return np.asarray(x).astype(np.float64)


def striped(idx):
    return np.tile(idx.reshape(-1, 16).T, (8, 1)).astype(np.uint16)


def unstriped(offs):
    return offs[:16].T.reshape(-1).astype(np.int64)


E2M1 = np.array([0.0, 0.5, 1.0, 1.5, 2.0, 3.0, 4.0, 6.0, -0.0, -0.5, -1.0, -1.5, -2.0, -3.0, -4.0, -6.0])


def pack_weight(w, fmt):
    k, n = w.shape
    w = f64(np.asarray(w, np.float32).astype(ml_dtypes.bfloat16)).reshape(k // 32, 32, n)
    amax = np.abs(w).max(1)
    if fmt == "e4m3":
        byte = np.frexp(amax)[1] - 1 + 127 - 7
    else:
        mant, ex = np.frexp(amax / 6.0)
        byte = np.where(mant > 0.5, ex, ex - 1) + 127
    byte = np.clip(np.where(amax > 0, byte, 1), 1, 254)
    scaled = (w * np.exp2(127.0 - byte)[:, None, :]).reshape(k, n).astype(np.float32)
    by_word = np.ascontiguousarray(scaled.reshape(k // 512, 128, 4, n).transpose(0, 1, 3, 2))
    if fmt == "e4m3":
        words = by_word.astype(ml_dtypes.float8_e4m3fn).view(np.uint8)
    else:
        c = by_word.astype(ml_dtypes.float4_e2m1fn).view(np.uint8) & 0xF
        words = (c[..., 0::2] | (c[..., 1::2] << 4)).reshape(k // 512, 128, 2 * n)
    return np.ascontiguousarray(words), np.ascontiguousarray(byte.astype(np.uint8).reshape(k // 512, 16, n))


def unpack_weight(words, scales, fmt):
    g, _, n = scales.shape
    words = np.ascontiguousarray(words).reshape(g, 128, n, -1)
    if fmt == "e4m3":
        vals = words.view(ml_dtypes.float8_e4m3fn).astype(np.float64)
    else:
        nib = np.empty((g, 128, n, 4), np.uint8)
        nib[..., 0::2] = words & 0xF
        nib[..., 1::2] = words >> 4
        vals = E2M1[nib]
    vals = vals * np.repeat(np.exp2(scales.astype(np.float64) - 127.0), 8, axis=1)[..., None]
    return vals.transpose(0, 1, 3, 2).reshape(g * 512, n)


def gelu(v):
    return 0.5 * v * (1.0 + np.tanh(np.sqrt(2.0 / np.pi) * (v + 0.044715 * v**3)))


def twice(P):
    return np.random.permutation(np.repeat(np.arange(P), 2))


K, H, T, S, P = 1024, 1024, 4096, 1024, 512

def setup_inputs():
    n = np.random.standard_normal
    s = mx_kscale(K)[:, None]
    u = mx_kscale(H)[:, None]
    d = {}
    d["tab_words"], d["tab_scales"] = pack_weight(n((K, T)) * s, "e4m3")
    d["offs"] = striped(np.random.permutation(T)[:S])
    d["pos1"] = striped(np.random.permutation(S)[:P])
    d["pos2"] = striped(np.random.permutation(S)[:P])
    d["pos3"] = striped(twice(P))
    d["w1"] = (n((K, H)) / s * u.T / K**0.5).astype(np.float32)
    d["w4_words"], d["w4_scales"] = pack_weight(n((K, H)) / s / K**0.5, "e2m1")
    d["b4"] = (0.5 * n(H)).astype(np.float32)
    d["w2"] = (n((H, H)) / u / H**0.5).astype(np.float32)
    d["gain"] = (np.exp(0.3 * n(H)) / u[:, 0]).astype(np.float32)
    d["base"] = (0.5 * n(H)).astype(np.float32)
    return d

def reference(tab_words, tab_scales, offs, pos1, pos2, pos3, w1, w4_words, w4_scales, b4, w2, gain, base):
    v = unpack_weight(tab_words, tab_scales, "e4m3")[:, unstriped(offs)]
    w4 = unpack_weight(w4_words, w4_scales, "e2m1")
    a = mxq(f64(w1), 0, "e4m3").T @ v
    b = (w4.T @ v) + f64(b4)[:, None]
    h = a * b
    x = np.minimum(h[:, unstriped(pos1)], h[:, unstriped(pos2)])
    y = mxq(f64(w2), 0, "e4m3").T @ mxq(x, 0, "e4m3")
    up = y[:, unstriped(pos3)]
    own = f64(gain)[:, None] * h
    return np.abs(up - own) + f64(base)[:, None]

@@ -1,0 +1,262 @@
+from contextlib import ExitStack
+
+import concourse.mybir as mybir
+
+K, H, T, S, R = 1024, 1024, 4096, 1024, 512
+FLOPS = 2 * K * H * S * 2 + 2 * H * H * R
+
+F32 = mybir.dt.float32
+BF16 = mybir.dt.bfloat16
+I32 = mybir.dt.int32
+U32 = mybir.dt.uint32
+U16 = mybir.dt.uint16
+U8 = mybir.dt.uint8
+FP8X4 = mybir.dt.float8_e4m3fn_x4
+FP4X4 = mybir.dt.float4_e2m1fn_x4
+ALU = mybir.AluOpType
+ACT = mybir.ActivationFunctionType
+
+P = 128
+PACK = 4
+PASS = P * PACK
+PASSES = K // PASS
+BANK = 512
+TILES = H // P
+Y_WINDOW = S + 16
+BASE_ON_VECTOR = (2, 5, 7)
+
+
+def tile_list_ridge_region_scorer_kernel(
+    tc, tab_words, tab_scales, offs, pos1, pos2, pos3, w1, w4_words, w4_scales, b4, w2, gain, base, out
+):
+    nc = tc.nc
+    with ExitStack() as ctx:
+        keep = ctx.enter_context(tc.tile_pool(name="keep", bufs=1))
+        ring = ctx.enter_context(tc.tile_pool(name="ring", bufs=1))
+        psum = ctx.enter_context(tc.psum_pool(name="psum", bufs=1))
+
+        def load_list(name, src):
+            t = keep.tile(list(src.shape), U16, name=name)
+            nc.sync.dma_start(t[:], src)
+            return t
+
+        tab_s = keep.tile([P, PASSES, T], U8, name="tab_s", align_bytes=64)
+        nc.vector.memset(tab_s[:].rearrange("p a t -> p (a t)").bitcast(I32), 0)
+        w4_s_raw = keep.tile([P, PASSES, H], U8, name="w4_s_raw", align_bytes=64)
+        nc.vector.memset(w4_s_raw[:].rearrange("p a c -> p (a c)").bitcast(I32), 0)
+
+        w4_raw = ring.tile([P, PASSES, 2 * H], U8, name="w4_raw", tag="early", bufs=1, align_bytes=64)
+        nc.sync.dma_start(w4_raw[:].bitcast(I32), w4_words.rearrange("a p c -> p a c").bitcast(I32))
+        offs_sb = load_list("offs_sb", offs)
+        pos1_sb = load_list("pos1_sb", pos1)
+        pos2_sb = load_list("pos2_sb", pos2)
+        pos3_sb = load_list("pos3_sb", pos3)
+
+        for q in range(4):
+            nc.gpsimd.dma_start(
+                w4_s_raw[32 * q : 32 * q + 4, :, :].bitcast(I32),
+                w4_scales[:, 4 * q : 4 * q + 4, :].rearrange("a r c -> r a c").bitcast(I32),
+            )
+        for q in range(4):
+            nc.scalar.dma_start(
+                tab_s[32 * q : 32 * q + 4, :, :].bitcast(I32),
+                tab_scales[:, 4 * q : 4 * q + 4, :].rearrange("a r t -> r a t").bitcast(I32),
+            )
+        tab = []
+        for a in range(PASSES):
+            t = keep.tile([P, T], I32, name="tab%d" % a, align_bytes=64)
+            nc.sync.dma_start(t[:], tab_words[a].rearrange("p t i -> p (t i)").bitcast(I32))
+            tab.append(t)
+
+        y_win = [keep.tile([P, Y_WINDOW], F32, name="y_win%d" % i, align_bytes=64) for i in range(3)]
+        nc.vector.memset(y_win[0][:, R:], 0.0)
+        for i in (1, 2):
+            nc.scalar.activation(y_win[i][:, R:], y_win[0][:, R:], ACT.Identity)
+
+        w4_q = keep.tile([P, PASSES, 2 * H], U8, name="w4_q", align_bytes=64)
+        nc.vector.tensor_copy(
+            w4_q[:].rearrange("p a (b t m e) -> p (a b) t m e", b=2, t=PACK, e=2),
+            w4_raw[:].rearrange("p a (b m t e) -> p (a b) t m e", b=2, t=PACK, e=2),
+        )
+        w4_s = keep.tile([P, PASSES, H], U8, name="w4_s", align_bytes=64)
+        nc.vector.tensor_copy(
+            w4_s[:].rearrange("p a (b t m) -> p (a b) t m", b=2, t=PACK),
+            w4_s_raw[:].rearrange("p a (b m t) -> p (a b) t m", b=2, t=PACK),
+        )
+
+        vecs = ring.tile([P, 3, PASSES, PACK], F32, name="vecs", tag="early", bufs=1, align_bytes=64)
+        for i, src in enumerate((b4, gain, base)):
+            nc.sync.dma_start(vecs[:, i], src.rearrange("(b p t) -> p b t", p=P, t=PACK))
+        b4_sb, gain_sb, base_sb = vecs[:, 0], vecs[:, 1], vecs[:, 2]
+
+        v_q = [keep.tile([P, S], U32, name="v_q%d" % a, align_bytes=64) for a in range(PASSES)]
+        v_s = [keep.tile([P, S], U8, name="v_s%d" % a, align_bytes=64) for a in range(PASSES)]
+        for a in range(PASSES):
+            nc.vector.tensor_copy(v_s[a][:], tab_s[:, a, :].indirect(offs_sb[:]))
+        nc.vector.tensor_copy(v_q[0][:], tab[0][:].bitcast(U32).indirect(offs_sb[:]))
+        for s in range(S // BANK):
+            nc.vector.tensor_copy(
+                v_q[1][:, s * BANK : (s + 1) * BANK],
+                tab[1][:].bitcast(U32).indirect(offs_sb[:, s * 32 : (s + 1) * 32]),
+            )
+
+        codes, scales, grouped = {}, {}, {}
+
+        def cast_weight(name, w, a, b, engine):
+            raw = ring.tile([P, PACK, PASS], F32, name="raw", tag="raw", bufs=2)
+            nc.sync.dma_start(
+                raw[:], w[a * PASS : (a + 1) * PASS, b * PASS : (b + 1) * PASS].rearrange("(p j) c -> p j c", j=PACK)
+            )
+            g = ring.tile([P, PACK, P, PACK], BF16, name="grouped", tag="grouped", bufs=3, align_bytes=64)
+            dst = g[:].rearrange("p t m j -> p m j t")
+            src = raw[:].rearrange("p j (m t) -> p m j t", t=PACK)
+            if engine == "vector":
+                nc.vector.tensor_copy(dst, src)
+            else:
+                nc.scalar.copy(dst, src)
+            grouped[name, a, b] = g
+
+        def quantise_weight(name, a, b):
+            c = keep.tile([P, PASS], U32, name="%s_q%d%d" % (name, a, b), align_bytes=64)
+            s = keep.tile([P, PASS], U8, name="%s_s%d%d" % (name, a, b), align_bytes=64)
+            nc.vector.quantize_mx(
+                out=c[:].bitcast(FP8X4), scales=s[:], in_=grouped[name, a, b][:].rearrange("p t m j -> p (t m j)")
+            )
+            codes[name, a, b], scales[name, a, b] = c, s
+
+        biased = {}
+
+        def product_b(n):
+            b, t = divmod(n, PACK)
+            bb = ring.tile([P, S], F32, name="bb", tag="bb", bufs=3)
+            for s in range(S // BANK):
+                cols = slice(s * BANK, (s + 1) * BANK)
+                acc = psum.tile([P, BANK], F32, name="acc_b", tag="acc_b", bufs=2)
+                for a in range(PASSES):
+                    nc.tensor.matmul_mx(
+                        out=acc[:],
+                        lhsT=w4_q[:, a, 2 * P * n : 2 * P * (n + 1)].bitcast(FP4X4),
+                        lhsT_scale=w4_s[:, a, P * n : P * (n + 1)],
+                        rhs=v_q[a][:, cols].bitcast(FP8X4),
+                        rhs_scale=v_s[a][:, cols],
+                        start=(a == 0),
+                        stop=(a == PASSES - 1),
+                    )
+                nc.scalar.activation(bb[:, cols], acc[:], ACT.Identity, bias=b4_sb[:, b, t : t + 1])
+            biased[n] = bb
+
+        feats, own = {}, {}
+
+        def product_a(n):
+            b, t = divmod(n, PACK)
+            h = ring.tile([P, S], F32, name="h", tag="row", bufs=4)
+            for s in range(S // BANK):
+                cols = slice(s * BANK, (s + 1) * BANK)
+                acc = psum.tile([P, BANK], F32, name="acc_a", tag="acc_a", bufs=4)
+                for a in range(PASSES):
+                    nc.tensor.matmul_mx(
+                        out=acc[:],
+                        lhsT=codes["w1", a, b][:, P * t : P * (t + 1)].bitcast(FP8X4),
+                        lhsT_scale=scales["w1", a, b][:, P * t : P * (t + 1)],
+                        rhs=v_q[a][:, cols].bitcast(FP8X4),
+                        rhs_scale=v_s[a][:, cols],
+                        start=(a == 0),
+                        stop=(a == PASSES - 1),
+                    )
+                nc.vector.tensor_tensor(h[:, cols], acc[:], biased[n][:, cols], ALU.mult)
+            feats[n] = h
+
+        picked = {}
+
+        def pick_pairs(n):
+            b, t = divmod(n, PACK)
+            if t == 0:
+                picked[1] = ring.tile([P, PACK, R], F32, name="pick1", tag="pick1", bufs=1)
+                picked[2] = ring.tile([P, PACK, R], F32, name="pick2", tag="pick2", bufs=1)
+            nc.vector.tensor_copy(picked[1][:, t, :], feats[n][:].indirect(pos1_sb[:]))
+            nc.vector.tensor_copy(picked[2][:, t, :], feats[n][:].indirect(pos2_sb[:]))
+            o = keep.tile([P, S], F32, name="own%d" % n)
+            nc.scalar.activation(o[:], feats[n][:], ACT.Copy, scale=gain_sb[:, b, t : t + 1])
+            own[n] = o
+
+        x_b = {}
+
+        def lesser(b):
+            x = ring.tile([P, R, PACK], BF16, name="x_b", tag="x_b", bufs=2, align_bytes=64)
+            nc.vector.tensor_tensor(
+                x[:].rearrange("p (c i) t -> p c t i", i=4),
+                picked[1][:].rearrange("p t (c i) -> p c t i", i=4),
+                picked[2][:].rearrange("p t (c i) -> p c t i", i=4),
+                ALU.min,
+            )
+            x_b[b] = x
+
+        def quantise_x(b):
+            c = keep.tile([P, R], U32, name="x_q%d" % b, align_bytes=64)
+            s = keep.tile([P, R], U8, name="x_s%d" % b, align_bytes=64)
+            nc.vector.quantize_mx(out=c[:].bitcast(FP8X4), scales=s[:], in_=x_b[b][:].rearrange("p m t -> p (m t)"))
+            codes["x", b], scales["x", b] = c, s
+
+        out_rows = out.rearrange("(b p t) j -> b t p j", p=P, t=PACK)
+
+        def product_y(n):
+            b, t = divmod(n, PACK)
+            acc = psum.tile([P, R], F32, name="acc_y", tag="acc_y", bufs=2)
+            for a in range(PASSES):
+                nc.tensor.matmul_mx(
+                    out=acc[:],
+                    lhsT=codes["w2", a, b][:, P * t : P * (t + 1)].bitcast(FP8X4),
+                    lhsT_scale=scales["w2", a, b][:, P * t : P * (t + 1)],
+                    rhs=codes["x", a][:].bitcast(FP8X4),
+                    rhs_scale=scales["x", a][:],
+                    start=(a == 0),
+                    stop=(a == PASSES - 1),
+                )
+            nc.scalar.activation(y_win[n % 3][:, :R], acc[:], ACT.Copy, scale=-1.0)
+
+        def score(n, pieces):
+            b, t = divmod(n, PACK)
+            d = ring.tile([P, S], F32, name="d", tag="row", bufs=4)
+            width = S // pieces
+            for i in range(pieces):
+                cols = slice(i * width, (i + 1) * width)
+                lst = pos3_sb[:, i * width // 16 : (i + 1) * width // 16]
+                nc.vector.tensor_tensor(d[:, cols], y_win[n % 3][:].indirect(lst), own[n][:, cols], ALU.add)
+            for i in range(pieces):
+                cols = slice(i * width, (i + 1) * width)
+                nc.scalar.activation(d[:, cols], d[:, cols], ACT.Abs)
+                if n in BASE_ON_VECTOR:
+                    nc.vector.tensor_scalar_add(d[:, cols], d[:, cols], base_sb[:, b, t : t + 1])
+                else:
+                    nc.scalar.activation(d[:, cols], d[:, cols], ACT.Identity, bias=base_sb[:, b, t : t + 1])
+                nc.sync.dma_start(out_rows[b, t][:, cols], d[:, cols])
+
+        product_b(0)
+        cast_weight("w1", w1, 0, 0, "vector")
+        cast_weight("w1", w1, 1, 0, "vector")
+        quantise_weight("w1", 0, 0)
+        quantise_weight("w1", 1, 0)
+        later = [("w1", w1, 0, 1), ("w1", w1, 1, 1), ("w2", w2, 0, 0), ("w2", w2, 1, 0), ("w2", w2, 0, 1), ("w2", w2, 1, 1)]
+        for n in range(TILES):
+            if n + 1 < TILES:
+                product_b(n + 1)
+            product_a(n)
+            if n < len(later):
+                cast_weight(*later[n], "scalar")
+            if n == PACK + 1:
+                quantise_x(0)
+            if n == PACK:
+                lesser(0)
+            pick_pairs(n)
+            if 1 <= n <= 4:
+                quantise_weight(later[n - 1][0], later[n - 1][2], later[n - 1][3])
+        lesser(1)
+        quantise_weight("w2", 0, 1)
+        quantise_x(1)
+        quantise_weight("w2", 1, 1)
+        product_y(0)
+        product_y(1)
+        for n in range(TILES):
+            if n + 2 < TILES:
+                product_y(n + 2)
+            score(n, 2 if n == TILES - 1 else 1)

@@ -1,6 +1,7 @@
 from contextlib import ExitStack
 
 import concourse.mybir as mybir
+from concourse.masks import make_identity
 
 K, H, T, S, R = 1024, 1024, 4096, 1024, 512
 FLOPS = 2 * K * H * S * 2 + 2 * H * H * R
@@ -24,6 +25,7 @@ BANK = 512
 TILES = H // P
 Y_WINDOW = S + 16
 BASE_ON_VECTOR = (2, 5, 7)
+OWN_ON_VECTOR = (7,)
 
 
 def tile_list_ridge_region_scorer_kernel(
@@ -33,6 +35,7 @@ def tile_list_ridge_region_scorer_kernel(
     with ExitStack() as ctx:
         keep = ctx.enter_context(tc.tile_pool(name="keep", bufs=1))
         ring = ctx.enter_context(tc.tile_pool(name="ring", bufs=1))
+        head = ctx.enter_context(tc.tile_pool(name="head", bufs=1))
         psum = ctx.enter_context(tc.psum_pool(name="psum", bufs=1))
 
         def load_list(name, src):
@@ -40,183 +43,213 @@ def tile_list_ridge_region_scorer_kernel(
             nc.sync.dma_start(t[:], src)
             return t
 
-        tab_s = keep.tile([P, PASSES, T], U8, name="tab_s", align_bytes=64)
-        nc.vector.memset(tab_s[:].rearrange("p a t -> p (a t)").bitcast(I32), 0)
-        w4_s_raw = keep.tile([P, PASSES, H], U8, name="w4_s_raw", align_bytes=64)
-        nc.vector.memset(w4_s_raw[:].rearrange("p a c -> p (a c)").bitcast(I32), 0)
+        def load_scale_rows(t, src):
+            nc.sync.dma_start(t[0:32, :].bitcast(I32), src.rearrange("a q c -> (a q) c").bitcast(I32))
+            nc.vector.memset(t[32:64, :].bitcast(I32), 0)
+            nc.vector.memset(t[64:P, :].bitcast(I32), 0)
+            return t
 
-        w4_raw = ring.tile([P, PASSES, 2 * H], U8, name="w4_raw", tag="early", bufs=1, align_bytes=64)
-        nc.sync.dma_start(w4_raw[:].bitcast(I32), w4_words.rearrange("a p c -> p a c").bitcast(I32))
+        def load_table(t, a):
+            nc.sync.dma_start(t[:], tab_words[a].rearrange("p t i -> p (t i)").bitcast(I32))
+            return t
+
+        def load_weight(raw, w, a, c0):
+            cols = slice(c0, c0 + raw[:].shape[2])
+            nc.sync.dma_start(raw[:], w[a * PASS : (a + 1) * PASS, cols].rearrange("(p j) c -> p j c", j=PACK))
+            return raw
+
+        ident = keep.tile([P, P], F32, name="ident")
+        make_identity(nc, ident[:])
+        vec_rows = keep.tile([P, PASS], F32, name="vec_rows")
+        nc.vector.memset(vec_rows[:], 0.0)
+
+        tab_s = load_scale_rows(keep.tile([P, T], U8, name="tab_s", align_bytes=64), tab_scales)
         offs_sb = load_list("offs_sb", offs)
+        w4_s_raw = load_scale_rows(keep.tile([P, H], U8, name="w4_s_raw", align_bytes=64), w4_scales)
+        w4_raw = keep.tile([P, PASSES, 2 * H], U8, name="w4_raw", align_bytes=64)
+        nc.sync.dma_start(w4_raw[:].bitcast(I32), w4_words.rearrange("a p c -> p a c").bitcast(I32))
         pos1_sb = load_list("pos1_sb", pos1)
         pos2_sb = load_list("pos2_sb", pos2)
         pos3_sb = load_list("pos3_sb", pos3)
+        tab = [load_table(keep.tile([P, T], I32, name="tab0", align_bytes=64), 0)]
+        first_raw = [load_weight(keep.tile([P, PACK, P], F32, name="first%d" % a), w1, a, 0) for a in range(PASSES)]
 
-        for q in range(4):
-            nc.gpsimd.dma_start(
-                w4_s_raw[32 * q : 32 * q + 4, :, :].bitcast(I32),
-                w4_scales[:, 4 * q : 4 * q + 4, :].rearrange("a r c -> r a c").bitcast(I32),
-            )
-        for q in range(4):
-            nc.scalar.dma_start(
-                tab_s[32 * q : 32 * q + 4, :, :].bitcast(I32),
-                tab_scales[:, 4 * q : 4 * q + 4, :].rearrange("a r t -> r a t").bitcast(I32),
-            )
-        tab = []
-        for a in range(PASSES):
-            t = keep.tile([P, T], I32, name="tab%d" % a, align_bytes=64)
-            nc.sync.dma_start(t[:], tab_words[a].rearrange("p t i -> p (t i)").bitcast(I32))
-            tab.append(t)
+        for i, src in enumerate((b4, gain, base)):
+            nc.gpsimd.dma_start(vec_rows[2 * i : 2 * i + 2, :], src.rearrange("(b c) -> b c", b=2))
+        vecs = keep.tile([P, 2, PACK, 3], F32, name="vecs")
+        for b in range(2):
+            turned = psum.tile([P, PACK, P], F32, name="turned", tag="acc_y", bufs=2)
+            for t in range(PACK):
+                src = vec_rows[:, t * P : (t + 1) * P] if b == 0 else vec_rows[:, t:PASS:PACK]
+                nc.tensor.transpose(turned[:, t, :], src, ident[:])
+            nc.scalar.activation(vecs[:, b], turned[:, :, b:6:2], ACT.Identity)
+
+        def vec(i, n):
+            return vecs[:, n // PACK, n % PACK, i : i + 1]
 
         y_win = [keep.tile([P, Y_WINDOW], F32, name="y_win%d" % i, align_bytes=64) for i in range(3)]
-        nc.vector.memset(y_win[0][:, R:], 0.0)
-        for i in (1, 2):
-            nc.scalar.activation(y_win[i][:, R:], y_win[0][:, R:], ACT.Identity)
+        for t in y_win:
+            nc.gpsimd.memset(t[:, R:], 0.0)
 
-        w4_q = keep.tile([P, PASSES, 2 * H], U8, name="w4_q", align_bytes=64)
+        planes = keep.tile([P, PASSES, S + H], U8, name="planes", align_bytes=64)
+        nc.vector.memset(planes[:, 1, :].bitcast(I32), 0)
+        picked_s = head.tile([P, 12 * S], U8, name="picked_s", offset=5120, align_bytes=64)[:, :S]
+        nc.vector.tensor_copy(picked_s, tab_s[:].indirect(offs_sb[:]))
+        nc.vector.tensor_copy(planes[:, 0, S : S + PASS].bitcast(I32), w4_s_raw[:, :PASS].bitcast(I32))
         nc.vector.tensor_copy(
-            w4_q[:].rearrange("p a (b t m e) -> p (a b) t m e", b=2, t=PACK, e=2),
-            w4_raw[:].rearrange("p a (b m t e) -> p (a b) t m e", b=2, t=PACK, e=2),
+            planes[:, 0, S + PASS :].rearrange("p (t m) -> p t m", t=PACK),
+            w4_s_raw[:, PASS:].rearrange("p (m t) -> p t m", t=PACK),
         )
-        w4_s = keep.tile([P, PASSES, H], U8, name="w4_s", align_bytes=64)
+        nc.vector.tensor_copy(planes[:, 0, :S].bitcast(I32), picked_s.bitcast(I32))
+
+        def move_scale_rows(a, q):
+            row = 16 * a + 4 * q
+            nc.sync.dma_start(planes[32 * q : 32 * q + 4, a, :].bitcast(I32), planes[row : row + 4, 0, :].bitcast(I32))
+
+        for q in range(1, 4):
+            move_scale_rows(0, q)
+        tab.append(load_table(head.tile([P, T], I32, name="tab1", offset=16384, align_bytes=64), 1))
+        for q in range(4):
+            move_scale_rows(1, q)
+        rest = PASS - P
+        rest_raw = [
+            load_weight(head.tile([P, PACK, rest], F32, name="rest%d" % a, offset=6144 * a), w1, a, P)
+            for a in range(PASSES)
+        ]
+
+        w4_dealt = keep.tile([P, PASSES, H], U8, name="w4_dealt", align_bytes=64)
         nc.vector.tensor_copy(
-            w4_s[:].rearrange("p a (b t m) -> p (a b) t m", b=2, t=PACK),
-            w4_s_raw[:].rearrange("p a (b m t) -> p (a b) t m", b=2, t=PACK),
+            w4_dealt[:].bitcast(U16).rearrange("p a (t m) -> p a t m", t=PACK),
+            w4_raw[:, :, H:].bitcast(U16).rearrange("p a (m t) -> p a t m", t=PACK),
         )
 
-        vecs = ring.tile([P, 3, PASSES, PACK], F32, name="vecs", tag="early", bufs=1, align_bytes=64)
-        for i, src in enumerate((b4, gain, base)):
-            nc.sync.dma_start(vecs[:, i], src.rearrange("(b p t) -> p b t", p=P, t=PACK))
-        b4_sb, gain_sb, base_sb = vecs[:, 0], vecs[:, 1], vecs[:, 2]
+        codes, scales, grouped = {}, {}, {}
+
+        def cast_plain(key, raw_cols):
+            width = raw_cols.shape[2]
+            g = ring.tile([P, width, PACK], BF16, name="grouped", tag="grouped", bufs=4, align_bytes=64)
+            nc.scalar.copy(
+                g[:].rearrange("p (c i) j -> p c j i", i=4), raw_cols.rearrange("p j (c i) -> p c j i", i=4)
+            )
+            grouped[key] = g[:].rearrange("p m j -> p (m j)")
+
+        def cast_dealt(key, raw):
+            g = ring.tile([P, PACK, P, PACK], BF16, name="grouped", tag="grouped", bufs=4, align_bytes=64)
+            nc.scalar.copy(g[:].rearrange("p t m j -> p m j t"), raw[:].rearrange("p j (m t) -> p m j t", t=PACK))
+            grouped[key] = g[:].rearrange("p t m j -> p (t m j)")
+
+        def quantise(key, first_tile):
+            src = grouped[key]
+            width = src.shape[1] // PACK
+            name = "%s_%d_%d" % key
+            c = keep.tile([P, width], U32, name=name + "_q", align_bytes=64)
+            s = keep.tile([P, width], U8, name=name + "_s", align_bytes=64)
+            nc.vector.quantize_mx(out=c[:].bitcast(FP8X4), scales=s[:], in_=src)
+            for i in range(width // P):
+                codes[key[0], key[1], first_tile + i] = c[:, i * P : (i + 1) * P].bitcast(FP8X4)
+                scales[key[0], key[1], first_tile + i] = s[:, i * P : (i + 1) * P]
+            return c, s
 
         v_q = [keep.tile([P, S], U32, name="v_q%d" % a, align_bytes=64) for a in range(PASSES)]
-        v_s = [keep.tile([P, S], U8, name="v_s%d" % a, align_bytes=64) for a in range(PASSES)]
-        for a in range(PASSES):
-            nc.vector.tensor_copy(v_s[a][:], tab_s[:, a, :].indirect(offs_sb[:]))
         nc.vector.tensor_copy(v_q[0][:], tab[0][:].bitcast(U32).indirect(offs_sb[:]))
+        for a in range(PASSES):
+            cast_plain(("w1", a, 0), first_raw[a][:])
+            quantise(("w1", a, 0), 0)
         for s in range(S // BANK):
             nc.vector.tensor_copy(
                 v_q[1][:, s * BANK : (s + 1) * BANK],
                 tab[1][:].bitcast(U32).indirect(offs_sb[:, s * 32 : (s + 1) * 32]),
             )
 
-        codes, scales, grouped = {}, {}, {}
+        plain, feats, own = {}, {}, {}
 
-        def cast_weight(name, w, a, b, engine):
-            raw = ring.tile([P, PACK, PASS], F32, name="raw", tag="raw", bufs=2)
-            nc.sync.dma_start(
-                raw[:], w[a * PASS : (a + 1) * PASS, b * PASS : (b + 1) * PASS].rearrange("(p j) c -> p j c", j=PACK)
-            )
-            g = ring.tile([P, PACK, P, PACK], BF16, name="grouped", tag="grouped", bufs=3, align_bytes=64)
-            dst = g[:].rearrange("p t m j -> p m j t")
-            src = raw[:].rearrange("p j (m t) -> p m j t", t=PACK)
-            if engine == "vector":
-                nc.vector.tensor_copy(dst, src)
-            else:
-                nc.scalar.copy(dst, src)
-            grouped[name, a, b] = g
-
-        def quantise_weight(name, a, b):
-            c = keep.tile([P, PASS], U32, name="%s_q%d%d" % (name, a, b), align_bytes=64)
-            s = keep.tile([P, PASS], U8, name="%s_s%d%d" % (name, a, b), align_bytes=64)
-            nc.vector.quantize_mx(
-                out=c[:].bitcast(FP8X4), scales=s[:], in_=grouped[name, a, b][:].rearrange("p t m j -> p (t m j)")
-            )
-            codes[name, a, b], scales[name, a, b] = c, s
-
-        biased = {}
-
-        def product_b(n):
+        def product_b(n, s):
             b, t = divmod(n, PACK)
-            bb = ring.tile([P, S], F32, name="bb", tag="bb", bufs=3)
-            for s in range(S // BANK):
-                cols = slice(s * BANK, (s + 1) * BANK)
-                acc = psum.tile([P, BANK], F32, name="acc_b", tag="acc_b", bufs=2)
-                for a in range(PASSES):
-                    nc.tensor.matmul_mx(
-                        out=acc[:],
-                        lhsT=w4_q[:, a, 2 * P * n : 2 * P * (n + 1)].bitcast(FP4X4),
-                        lhsT_scale=w4_s[:, a, P * n : P * (n + 1)],
-                        rhs=v_q[a][:, cols].bitcast(FP8X4),
-                        rhs_scale=v_s[a][:, cols],
-                        start=(a == 0),
-                        stop=(a == PASSES - 1),
-                    )
-                nc.scalar.activation(bb[:, cols], acc[:], ACT.Identity, bias=b4_sb[:, b, t : t + 1])
-            biased[n] = bb
+            if s == 0:
+                feats[n] = ring.tile([P, S], F32, name="h", tag="row", bufs=5)
+            cols = slice(s * BANK, (s + 1) * BANK)
+            acc = psum.tile([P, BANK], F32, name="acc_b", tag="acc_b", bufs=4)
+            words = w4_dealt if b else w4_raw
+            for a in range(PASSES):
+                nc.tensor.matmul_mx(
+                    out=acc[:],
+                    lhsT=words[:, a, 2 * P * t : 2 * P * (t + 1)].bitcast(FP4X4),
+                    lhsT_scale=planes[:, a, S + P * n : S + P * (n + 1)],
+                    rhs=v_q[a][:, cols].bitcast(FP8X4),
+                    rhs_scale=planes[:, a, cols],
+                    start=(a == 0),
+                    stop=(a == PASSES - 1),
+                )
+            nc.vector.scalar_tensor_tensor(feats[n][:, cols], acc[:], vec(0, n), plain[n][:, cols], ALU.add, ALU.mult)
 
-        feats, own = {}, {}
+        def product_a(n, s):
+            if s == 0:
+                plain[n] = ring.tile([P, S], F32, name="a_sb", tag="a_sb", bufs=3)
+            cols = slice(s * BANK, (s + 1) * BANK)
+            acc = psum.tile([P, BANK], F32, name="acc_a", tag="acc_a", bufs=2)
+            for a in range(PASSES):
+                nc.tensor.matmul_mx(
+                    out=acc[:],
+                    lhsT=codes["w1", a, n],
+                    lhsT_scale=scales["w1", a, n],
+                    rhs=v_q[a][:, cols].bitcast(FP8X4),
+                    rhs_scale=planes[:, a, cols],
+                    start=(a == 0),
+                    stop=(a == PASSES - 1),
+                )
+            nc.scalar.copy(plain[n][:, cols], acc[:])
 
-        def product_a(n):
-            b, t = divmod(n, PACK)
-            h = ring.tile([P, S], F32, name="h", tag="row", bufs=4)
-            for s in range(S // BANK):
-                cols = slice(s * BANK, (s + 1) * BANK)
-                acc = psum.tile([P, BANK], F32, name="acc_a", tag="acc_a", bufs=4)
-                for a in range(PASSES):
-                    nc.tensor.matmul_mx(
-                        out=acc[:],
-                        lhsT=codes["w1", a, b][:, P * t : P * (t + 1)].bitcast(FP8X4),
-                        lhsT_scale=scales["w1", a, b][:, P * t : P * (t + 1)],
-                        rhs=v_q[a][:, cols].bitcast(FP8X4),
-                        rhs_scale=v_s[a][:, cols],
-                        start=(a == 0),
-                        stop=(a == PASSES - 1),
-                    )
-                nc.vector.tensor_tensor(h[:, cols], acc[:], biased[n][:, cols], ALU.mult)
-            feats[n] = h
-
-        picked = {}
+        picked = [keep.tile([P, PACK, R], F32, name="pick%d" % i) for i in range(2)]
+        x_rows = keep.tile([P, PACK, R], BF16, name="x_rows")
 
         def pick_pairs(n):
-            b, t = divmod(n, PACK)
-            if t == 0:
-                picked[1] = ring.tile([P, PACK, R], F32, name="pick1", tag="pick1", bufs=1)
-                picked[2] = ring.tile([P, PACK, R], F32, name="pick2", tag="pick2", bufs=1)
-            nc.vector.tensor_copy(picked[1][:, t, :], feats[n][:].indirect(pos1_sb[:]))
-            nc.vector.tensor_copy(picked[2][:, t, :], feats[n][:].indirect(pos2_sb[:]))
-            o = keep.tile([P, S], F32, name="own%d" % n)
-            nc.scalar.activation(o[:], feats[n][:], ACT.Copy, scale=gain_sb[:, b, t : t + 1])
-            own[n] = o
+            t = n % PACK
+            nc.vector.tensor_copy(picked[0][:, t, :], feats[n][:].indirect(pos1_sb[:]))
+            nc.vector.tensor_copy(picked[1][:, t, :], feats[n][:].indirect(pos2_sb[:]))
 
-        x_b = {}
+        def scale_own(n):
+            own[n] = keep.tile([P, S], F32, name="own%d" % n)
+            if n in OWN_ON_VECTOR:
+                nc.vector.tensor_scalar_mul(own[n][:], feats[n][:], vec(1, n))
+            else:
+                nc.scalar.activation(own[n][:], feats[n][:], ACT.Copy, scale=vec(1, n))
 
-        def lesser(b):
-            x = ring.tile([P, R, PACK], BF16, name="x_b", tag="x_b", bufs=2, align_bytes=64)
+        def lesser_plain(t):
+            x = ring.tile([P, R], BF16, name="x_tile", tag="x_tile", bufs=2)
+            nc.vector.tensor_tensor(x[:], picked[0][:, t, :], picked[1][:, t, :], ALU.min)
+            for j in range(PACK):
+                nc.sync.dma_start(x_rows[32 * t : 32 * t + 32, j, :], x[j:P:PACK, :])
+
+        def lesser_dealt():
+            x = ring.tile([P, R, PACK], BF16, name="grouped", tag="grouped", bufs=4, align_bytes=64)
             nc.vector.tensor_tensor(
-                x[:].rearrange("p (c i) t -> p c t i", i=4),
-                picked[1][:].rearrange("p t (c i) -> p c t i", i=4),
-                picked[2][:].rearrange("p t (c i) -> p c t i", i=4),
+                x[:].rearrange("p (c i) t -> p c t i", i=2),
+                picked[0][:].rearrange("p t (c i) -> p c t i", i=2),
+                picked[1][:].rearrange("p t (c i) -> p c t i", i=2),
                 ALU.min,
             )
-            x_b[b] = x
+            grouped["x", 1, 0] = x[:].rearrange("p m t -> p (m t)")
 
-        def quantise_x(b):
-            c = keep.tile([P, R], U32, name="x_q%d" % b, align_bytes=64)
-            s = keep.tile([P, R], U8, name="x_s%d" % b, align_bytes=64)
-            nc.vector.quantize_mx(out=c[:].bitcast(FP8X4), scales=s[:], in_=x_b[b][:].rearrange("p m t -> p (m t)"))
-            codes["x", b], scales["x", b] = c, s
-
-        out_rows = out.rearrange("(b p t) j -> b t p j", p=P, t=PACK)
+        out_rows = [out[P * t : P * (t + 1), :] for t in range(PACK)]
+        out_rows.extend([out[PASS:, :].rearrange("(p t) j -> t p j", t=PACK)[t] for t in range(PACK)])
+        x_mx = {}
 
         def product_y(n):
-            b, t = divmod(n, PACK)
             acc = psum.tile([P, R], F32, name="acc_y", tag="acc_y", bufs=2)
             for a in range(PASSES):
                 nc.tensor.matmul_mx(
                     out=acc[:],
-                    lhsT=codes["w2", a, b][:, P * t : P * (t + 1)].bitcast(FP8X4),
-                    lhsT_scale=scales["w2", a, b][:, P * t : P * (t + 1)],
-                    rhs=codes["x", a][:].bitcast(FP8X4),
-                    rhs_scale=scales["x", a][:],
+                    lhsT=codes["w2", a, n],
+                    lhsT_scale=scales["w2", a, n],
+                    rhs=x_mx[a][0][:].bitcast(FP8X4),
+                    rhs_scale=x_mx[a][1][:],
                     start=(a == 0),
                     stop=(a == PASSES - 1),
                 )
             nc.scalar.activation(y_win[n % 3][:, :R], acc[:], ACT.Copy, scale=-1.0)
 
         def score(n, pieces):
-            b, t = divmod(n, PACK)
-            d = ring.tile([P, S], F32, name="d", tag="row", bufs=4)
+            d = ring.tile([P, S], F32, name="d", tag="row", bufs=5)
             width = S // pieces
             for i in range(pieces):
                 cols = slice(i * width, (i + 1) * width)
@@ -226,37 +259,50 @@ def tile_list_ridge_region_scorer_kernel(
                 cols = slice(i * width, (i + 1) * width)
                 nc.scalar.activation(d[:, cols], d[:, cols], ACT.Abs)
                 if n in BASE_ON_VECTOR:
-                    nc.vector.tensor_scalar_add(d[:, cols], d[:, cols], base_sb[:, b, t : t + 1])
+                    nc.vector.tensor_scalar_add(d[:, cols], d[:, cols], vec(2, n))
                 else:
-                    nc.scalar.activation(d[:, cols], d[:, cols], ACT.Identity, bias=base_sb[:, b, t : t + 1])
-                nc.sync.dma_start(out_rows[b, t][:, cols], d[:, cols])
+                    nc.scalar.activation(d[:, cols], d[:, cols], ACT.Identity, bias=vec(2, n))
+                nc.sync.dma_start(out_rows[n][:, cols], d[:, cols])
 
-        product_b(0)
-        cast_weight("w1", w1, 0, 0, "vector")
-        cast_weight("w1", w1, 1, 0, "vector")
-        quantise_weight("w1", 0, 0)
-        quantise_weight("w1", 1, 0)
+        def stream_weight(name, w, a, b):
+            raw = load_weight(head.tile([P, PACK, PASS], F32, name="raw_%s_%d_%d" % (name, a, b), offset=16384 * b + 8192 * a), w, a, b * PASS)
+            if b:
+                cast_dealt((name, a, b * PACK), raw)
+            else:
+                cast_plain((name, a, 0), raw[:])
+
         later = [("w1", w1, 0, 1), ("w1", w1, 1, 1), ("w2", w2, 0, 0), ("w2", w2, 1, 0), ("w2", w2, 0, 1), ("w2", w2, 1, 1)]
         for n in range(TILES):
-            if n + 1 < TILES:
-                product_b(n + 1)
-            product_a(n)
-            if n < len(later):
-                cast_weight(*later[n], "scalar")
-            if n == PACK + 1:
-                quantise_x(0)
-            if n == PACK:
-                lesser(0)
+            for half in range(S // BANK):
+                product_a(n, half)
+                product_b(n, half)
+            if n >= 1:
+                scale_own(n - 1)
+            if n < 2:
+                c0, c1 = ((0, P), (P, rest))[n]
+                for a in range(PASSES):
+                    cast_plain(("w1", a, n + 1), rest_raw[a][:, :, c0:c1])
+                    quantise(("w1", a, n + 1), n + 1)
+            if 1 <= n <= len(later):
+                stream_weight(*later[n - 1])
+            if 1 <= n <= PACK:
+                lesser_plain(n - 1)
             pick_pairs(n)
-            if 1 <= n <= 4:
-                quantise_weight(later[n - 1][0], later[n - 1][2], later[n - 1][3])
-        lesser(1)
-        quantise_weight("w2", 0, 1)
-        quantise_x(1)
-        quantise_weight("w2", 1, 1)
+            if 2 <= n <= 5:
+                name, w, a, b = later[n - 2]
+                quantise((name, a, b * PACK), b * PACK)
+            if n == 5:
+                cast_plain(("x", 0, 0), x_rows[:])
+            if n == 6:
+                x_mx[0] = quantise(("x", 0, 0), 0)
+        lesser_dealt()
+        quantise(("w2", 0, PACK), PACK)
+        x_mx[1] = quantise(("x", 1, 0), 0)
+        quantise(("w2", 1, PACK), PACK)
+        scale_own(TILES - 1)
         product_y(0)
         product_y(1)
         for n in range(TILES):
             if n + 2 < TILES:
                 product_y(n + 2)
-            score(n, 2 if n == TILES - 1 else 1)
+            score(n, 4 if n == TILES - 1 else 1)

@@ -24,7 +24,7 @@ PASSES = K // PASS
 BANK = 512
 TILES = H // P
 Y_WINDOW = S + 16
-BASE_ON_VECTOR = (2, 5, 7)
+BASE_ON_VECTOR = (6, 1, 3)
 OWN_ON_VECTOR = (7,)
 
 
@@ -53,9 +53,13 @@ def tile_list_ridge_region_scorer_kernel(
             nc.sync.dma_start(t[:], tab_words[a].rearrange("p t i -> p (t i)").bitcast(I32))
             return t
 
-        def load_weight(raw, w, a, c0):
-            cols = slice(c0, c0 + raw[:].shape[2])
-            nc.sync.dma_start(raw[:], w[a * PASS : (a + 1) * PASS, cols].rearrange("(p j) c -> p j c", j=PACK))
+        def load_weight(raw, w, a, c0, dealt_rows=False):
+            rows = w[a * PASS : (a + 1) * PASS, c0 : c0 + raw[:].shape[2]]
+            if dealt_rows:
+                for i in range(PACK):
+                    nc.sync.dma_start(raw[i:P:PACK], rows.rearrange("(g j i) c -> i g j c", j=PACK, i=PACK)[i])
+            else:
+                nc.sync.dma_start(raw[:], rows.rearrange("(p j) c -> p j c", j=PACK))
             return raw
 
         ident = keep.tile([P, P], F32, name="ident")
@@ -76,12 +80,17 @@ def tile_list_ridge_region_scorer_kernel(
 
         for i, src in enumerate((b4, gain, base)):
             nc.gpsimd.dma_start(vec_rows[2 * i : 2 * i + 2, :], src.rearrange("(b c) -> b c", b=2))
+        vec_dealt = keep.tile([P, PASS], F32, name="vec_dealt")
+        nc.scalar.activation(
+            vec_dealt[:].rearrange("p (t g i) -> p t g i", t=PACK, i=PACK),
+            vec_rows[:].rearrange("p (g t i) -> p t g i", t=PACK, i=PACK),
+            ACT.Identity,
+        )
         vecs = keep.tile([P, 2, PACK, 3], F32, name="vecs")
         for b in range(2):
             turned = psum.tile([P, PACK, P], F32, name="turned", tag="acc_y", bufs=2)
             for t in range(PACK):
-                src = vec_rows[:, t * P : (t + 1) * P] if b == 0 else vec_rows[:, t:PASS:PACK]
-                nc.tensor.transpose(turned[:, t, :], src, ident[:])
+                nc.tensor.transpose(turned[:, t, :], (vec_rows, vec_dealt)[b][:, t * P : (t + 1) * P], ident[:])
             nc.scalar.activation(vecs[:, b], turned[:, :, b:6:2], ACT.Identity)
 
         def vec(i, n):
@@ -97,8 +106,8 @@ def tile_list_ridge_region_scorer_kernel(
         nc.vector.tensor_copy(picked_s, tab_s[:].indirect(offs_sb[:]))
         nc.vector.tensor_copy(planes[:, 0, S : S + PASS].bitcast(I32), w4_s_raw[:, :PASS].bitcast(I32))
         nc.vector.tensor_copy(
-            planes[:, 0, S + PASS :].rearrange("p (t m) -> p t m", t=PACK),
-            w4_s_raw[:, PASS:].rearrange("p (m t) -> p t m", t=PACK),
+            planes[:, 0, S + PASS :].bitcast(I32).rearrange("p (t g) -> p t g", t=PACK),
+            w4_s_raw[:, PASS:].bitcast(I32).rearrange("p (g t) -> p t g", t=PACK),
         )
         nc.vector.tensor_copy(planes[:, 0, :S].bitcast(I32), picked_s.bitcast(I32))
 
@@ -119,8 +128,8 @@ def tile_list_ridge_region_scorer_kernel(
 
         w4_dealt = keep.tile([P, PASSES, H], U8, name="w4_dealt", align_bytes=64)
         nc.vector.tensor_copy(
-            w4_dealt[:].bitcast(U16).rearrange("p a (t m) -> p a t m", t=PACK),
-            w4_raw[:, :, H:].bitcast(U16).rearrange("p a (m t) -> p a t m", t=PACK),
+            w4_dealt[:].bitcast(I32).rearrange("p a (t g e) -> p a t g e", t=PACK, e=2),
+            w4_raw[:, :, H:].bitcast(I32).rearrange("p a (g t e) -> p a t g e", t=PACK, e=2),
         )
 
         codes, scales, grouped = {}, {}, {}
@@ -135,7 +144,10 @@ def tile_list_ridge_region_scorer_kernel(
 
         def cast_dealt(key, raw):
             g = ring.tile([P, PACK, P, PACK], BF16, name="grouped", tag="grouped", bufs=4, align_bytes=64)
-            nc.scalar.copy(g[:].rearrange("p t m j -> p m j t"), raw[:].rearrange("p j (m t) -> p m j t", t=PACK))
+            nc.scalar.copy(
+                g[:].rearrange("p t (g i) j -> p t g j i", i=PACK),
+                raw[:].rearrange("p j (g t i) -> p t g j i", t=PACK, i=PACK),
+            )
             grouped[key] = g[:].rearrange("p t m j -> p (t m j)")
 
         def quantise(key, first_tile):
@@ -230,11 +242,18 @@ def tile_list_ridge_region_scorer_kernel(
             )
             grouped["x", 1, 0] = x[:].rearrange("p m t -> p (m t)")
 
-        out_rows = [out[P * t : P * (t + 1), :] for t in range(PACK)]
-        out_rows.extend([out[PASS:, :].rearrange("(p t) j -> t p j", t=PACK)[t] for t in range(PACK)])
+        out_dealt = out[PASS:, :].rearrange("(g t i) j -> t i g j", t=PACK, i=PACK)
+
+        def store(n, d, cols):
+            if n < PACK:
+                nc.sync.dma_start(out[P * n : P * (n + 1), cols], d[:, cols])
+            else:
+                for i in range(PACK):
+                    nc.sync.dma_start(out_dealt[n - PACK, i][:, cols], d[i:P:PACK, cols])
+
         x_mx = {}
 
-        def product_y(n):
+        def product_y(n, win):
             acc = psum.tile([P, R], F32, name="acc_y", tag="acc_y", bufs=2)
             for a in range(PASSES):
                 nc.tensor.matmul_mx(
@@ -246,15 +265,15 @@ def tile_list_ridge_region_scorer_kernel(
                     start=(a == 0),
                     stop=(a == PASSES - 1),
                 )
-            nc.scalar.activation(y_win[n % 3][:, :R], acc[:], ACT.Copy, scale=-1.0)
+            nc.scalar.activation(win[:, :R], acc[:], ACT.Copy, scale=-1.0)
 
-        def score(n, pieces):
+        def score(n, win, pieces):
             d = ring.tile([P, S], F32, name="d", tag="row", bufs=5)
             width = S // pieces
             for i in range(pieces):
                 cols = slice(i * width, (i + 1) * width)
                 lst = pos3_sb[:, i * width // 16 : (i + 1) * width // 16]
-                nc.vector.tensor_tensor(d[:, cols], y_win[n % 3][:].indirect(lst), own[n][:, cols], ALU.add)
+                nc.vector.tensor_tensor(d[:, cols], win[:].indirect(lst), own[n][:, cols], ALU.add)
             for i in range(pieces):
                 cols = slice(i * width, (i + 1) * width)
                 nc.scalar.activation(d[:, cols], d[:, cols], ACT.Abs)
@@ -262,47 +281,49 @@ def tile_list_ridge_region_scorer_kernel(
                     nc.vector.tensor_scalar_add(d[:, cols], d[:, cols], vec(2, n))
                 else:
                     nc.scalar.activation(d[:, cols], d[:, cols], ACT.Identity, bias=vec(2, n))
-                nc.sync.dma_start(out_rows[n][:, cols], d[:, cols])
+                store(n, d, cols)
 
-        def stream_weight(name, w, a, b):
-            raw = load_weight(head.tile([P, PACK, PASS], F32, name="raw_%s_%d_%d" % (name, a, b), offset=16384 * b + 8192 * a), w, a, b * PASS)
+        def stream_weight(slot, name, w, a, b):
+            raw = load_weight(head.tile([P, PACK, PASS], F32, name="raw_%s_%d_%d" % (name, a, b), offset=8192 * slot), w, a, b * PASS, name == "w2" and a == 1)
             if b:
                 cast_dealt((name, a, b * PACK), raw)
             else:
                 cast_plain((name, a, 0), raw[:])
 
-        later = [("w1", w1, 0, 1), ("w1", w1, 1, 1), ("w2", w2, 0, 0), ("w2", w2, 1, 0), ("w2", w2, 0, 1), ("w2", w2, 1, 1)]
+        later = [("w1", w1, 0, 1), ("w1", w1, 1, 1), ("w2", w2, 0, 1), ("w2", w2, 1, 1), ("w2", w2, 0, 0), ("w2", w2, 1, 0)]
         for n in range(TILES):
             for half in range(S // BANK):
                 product_a(n, half)
                 product_b(n, half)
-            if n >= 1:
-                scale_own(n - 1)
             if n < 2:
                 c0, c1 = ((0, P), (P, rest))[n]
                 for a in range(PASSES):
                     cast_plain(("w1", a, n + 1), rest_raw[a][:, :, c0:c1])
                     quantise(("w1", a, n + 1), n + 1)
+            if 2 <= n <= PACK + 1:
+                lesser_plain(n - 2)
+            if n >= 1:
+                pick_pairs(n - 1)
+                scale_own(n - 1)
             if 1 <= n <= len(later):
-                stream_weight(*later[n - 1])
-            if 1 <= n <= PACK:
-                lesser_plain(n - 1)
-            pick_pairs(n)
+                stream_weight((n + 1) % 4, *later[n - 1])
             if 2 <= n <= 5:
                 name, w, a, b = later[n - 2]
                 quantise((name, a, b * PACK), b * PACK)
-            if n == 5:
-                cast_plain(("x", 0, 0), x_rows[:])
             if n == 6:
+                cast_plain(("x", 0, 0), x_rows[:])
+            if n == 7:
                 x_mx[0] = quantise(("x", 0, 0), 0)
+        pick_pairs(TILES - 1)
+        quantise(("w2", 0, 0), 0)
         lesser_dealt()
-        quantise(("w2", 0, PACK), PACK)
+        quantise(("w2", 1, 0), 0)
         x_mx[1] = quantise(("x", 1, 0), 0)
-        quantise(("w2", 1, PACK), PACK)
         scale_own(TILES - 1)
-        product_y(0)
-        product_y(1)
-        for n in range(TILES):
-            if n + 2 < TILES:
-                product_y(n + 2)
-            score(n, 4 if n == TILES - 1 else 1)
+        order = [4, 5, 6, 7, 0, 1, 2, 3]
+        product_y(order[0], y_win[0])
+        product_y(order[1], y_win[1])
+        for i, n in enumerate(order):
+            if i + 2 < TILES:
+                product_y(order[i + 2], y_win[(i + 2) % 3])
+            score(n, y_win[i % 3], 4 if i == TILES - 1 else 1)

@@ -23,9 +23,13 @@ PASS = P * PACK
 PASSES = K // PASS
 BANK = 512
 TILES = H // P
+PER_COLUMN = 16
+QUADRANT = 32
 Y_WINDOW = S + 16
-BASE_ON_VECTOR = (6, 1, 3)
-OWN_ON_VECTOR = (7,)
+RAW_SLOT = 4 * PACK * PASS
+SCORE_ORDER = (4, 5, 6, 7, 0, 1, 2, 3)
+LAST_PIECES = 4
+BASE_ON_VECTOR = (3,)
 
 
 def tile_list_ridge_region_scorer_kernel(
@@ -102,7 +106,7 @@ def tile_list_ridge_region_scorer_kernel(
 
         planes = keep.tile([P, PASSES, S + H], U8, name="planes", align_bytes=64)
         nc.vector.memset(planes[:, 1, :].bitcast(I32), 0)
-        picked_s = head.tile([P, 12 * S], U8, name="picked_s", offset=5120, align_bytes=64)[:, :S]
+        picked_s = head.tile([P, 12 * S], U8, name="picked_s", offset=5 * S, align_bytes=64)[:, :S]
         nc.vector.tensor_copy(picked_s, tab_s[:].indirect(offs_sb[:]))
         nc.vector.tensor_copy(planes[:, 0, S : S + PASS].bitcast(I32), w4_s_raw[:, :PASS].bitcast(I32))
         nc.vector.tensor_copy(
@@ -113,16 +117,18 @@ def tile_list_ridge_region_scorer_kernel(
 
         def move_scale_rows(a, q):
             row = 16 * a + 4 * q
-            nc.sync.dma_start(planes[32 * q : 32 * q + 4, a, :].bitcast(I32), planes[row : row + 4, 0, :].bitcast(I32))
+            nc.sync.dma_start(
+                planes[QUADRANT * q : QUADRANT * q + 4, a, :].bitcast(I32), planes[row : row + 4, 0, :].bitcast(I32)
+            )
 
         for q in range(1, 4):
             move_scale_rows(0, q)
-        tab.append(load_table(head.tile([P, T], I32, name="tab1", offset=16384, align_bytes=64), 1))
+        tab.append(load_table(head.tile([P, T], I32, name="tab1", offset=2 * RAW_SLOT, align_bytes=64), 1))
         for q in range(4):
             move_scale_rows(1, q)
         rest = PASS - P
         rest_raw = [
-            load_weight(head.tile([P, PACK, rest], F32, name="rest%d" % a, offset=6144 * a), w1, a, P)
+            load_weight(head.tile([P, PACK, rest], F32, name="rest%d" % a, offset=4 * PACK * rest * a), w1, a, P)
             for a in range(PASSES)
         ]
 
@@ -150,54 +156,37 @@ def tile_list_ridge_region_scorer_kernel(
             )
             grouped[key] = g[:].rearrange("p t m j -> p (t m j)")
 
-        def quantise(key, first_tile):
+        def quantise(key):
             src = grouped[key]
             width = src.shape[1] // PACK
             name = "%s_%d_%d" % key
             c = keep.tile([P, width], U32, name=name + "_q", align_bytes=64)
             s = keep.tile([P, width], U8, name=name + "_s", align_bytes=64)
             nc.vector.quantize_mx(out=c[:].bitcast(FP8X4), scales=s[:], in_=src)
-            for i in range(width // P):
-                codes[key[0], key[1], first_tile + i] = c[:, i * P : (i + 1) * P].bitcast(FP8X4)
-                scales[key[0], key[1], first_tile + i] = s[:, i * P : (i + 1) * P]
             return c, s
+
+        def quantise_weight(key):
+            c, s = quantise(key)
+            name, a, first_tile = key
+            for i in range(c[:].shape[1] // P):
+                codes[name, a, first_tile + i] = c[:, i * P : (i + 1) * P].bitcast(FP8X4)
+                scales[name, a, first_tile + i] = s[:, i * P : (i + 1) * P]
 
         v_q = [keep.tile([P, S], U32, name="v_q%d" % a, align_bytes=64) for a in range(PASSES)]
         nc.vector.tensor_copy(v_q[0][:], tab[0][:].bitcast(U32).indirect(offs_sb[:]))
         for a in range(PASSES):
             cast_plain(("w1", a, 0), first_raw[a][:])
-            quantise(("w1", a, 0), 0)
-        for s in range(S // BANK):
-            nc.vector.tensor_copy(
-                v_q[1][:, s * BANK : (s + 1) * BANK],
-                tab[1][:].bitcast(U32).indirect(offs_sb[:, s * 32 : (s + 1) * 32]),
-            )
+            quantise_weight(("w1", a, 0))
+        for half in range(S // BANK):
+            entries = offs_sb[:, half * BANK // PER_COLUMN : (half + 1) * BANK // PER_COLUMN]
+            nc.vector.tensor_copy(v_q[1][:, half * BANK : (half + 1) * BANK], tab[1][:].bitcast(U32).indirect(entries))
 
-        plain, feats, own = {}, {}, {}
+        prod_w1, feats, own = {}, {}, {}
 
-        def product_b(n, s):
-            b, t = divmod(n, PACK)
-            if s == 0:
-                feats[n] = ring.tile([P, S], F32, name="h", tag="row", bufs=5)
-            cols = slice(s * BANK, (s + 1) * BANK)
-            acc = psum.tile([P, BANK], F32, name="acc_b", tag="acc_b", bufs=4)
-            words = w4_dealt if b else w4_raw
-            for a in range(PASSES):
-                nc.tensor.matmul_mx(
-                    out=acc[:],
-                    lhsT=words[:, a, 2 * P * t : 2 * P * (t + 1)].bitcast(FP4X4),
-                    lhsT_scale=planes[:, a, S + P * n : S + P * (n + 1)],
-                    rhs=v_q[a][:, cols].bitcast(FP8X4),
-                    rhs_scale=planes[:, a, cols],
-                    start=(a == 0),
-                    stop=(a == PASSES - 1),
-                )
-            nc.vector.scalar_tensor_tensor(feats[n][:, cols], acc[:], vec(0, n), plain[n][:, cols], ALU.add, ALU.mult)
-
-        def product_a(n, s):
-            if s == 0:
-                plain[n] = ring.tile([P, S], F32, name="a_sb", tag="a_sb", bufs=3)
-            cols = slice(s * BANK, (s + 1) * BANK)
+        def product_w1(n, half):
+            if half == 0:
+                prod_w1[n] = ring.tile([P, S], F32, name="a_sb", tag="a_sb", bufs=3)
+            cols = slice(half * BANK, (half + 1) * BANK)
             acc = psum.tile([P, BANK], F32, name="acc_a", tag="acc_a", bufs=2)
             for a in range(PASSES):
                 nc.tensor.matmul_mx(
@@ -209,7 +198,26 @@ def tile_list_ridge_region_scorer_kernel(
                     start=(a == 0),
                     stop=(a == PASSES - 1),
                 )
-            nc.scalar.copy(plain[n][:, cols], acc[:])
+            nc.scalar.copy(prod_w1[n][:, cols], acc[:])
+
+        def product_w4(n, half):
+            dealt, t = divmod(n, PACK)
+            if half == 0:
+                feats[n] = ring.tile([P, S], F32, name="h", tag="row", bufs=5)
+            cols = slice(half * BANK, (half + 1) * BANK)
+            acc = psum.tile([P, BANK], F32, name="acc_b", tag="acc_b", bufs=4)
+            words = w4_dealt if dealt else w4_raw
+            for a in range(PASSES):
+                nc.tensor.matmul_mx(
+                    out=acc[:],
+                    lhsT=words[:, a, 2 * P * t : 2 * P * (t + 1)].bitcast(FP4X4),
+                    lhsT_scale=planes[:, a, S + P * n : S + P * (n + 1)],
+                    rhs=v_q[a][:, cols].bitcast(FP8X4),
+                    rhs_scale=planes[:, a, cols],
+                    start=(a == 0),
+                    stop=(a == PASSES - 1),
+                )
+            nc.vector.scalar_tensor_tensor(feats[n][:, cols], acc[:], vec(0, n), prod_w1[n][:, cols], ALU.add, ALU.mult)
 
         picked = [keep.tile([P, PACK, R], F32, name="pick%d" % i) for i in range(2)]
         x_rows = keep.tile([P, PACK, R], BF16, name="x_rows")
@@ -221,7 +229,7 @@ def tile_list_ridge_region_scorer_kernel(
 
         def scale_own(n):
             own[n] = keep.tile([P, S], F32, name="own%d" % n)
-            if n in OWN_ON_VECTOR:
+            if n == TILES - 1:
                 nc.vector.tensor_scalar_mul(own[n][:], feats[n][:], vec(1, n))
             else:
                 nc.scalar.activation(own[n][:], feats[n][:], ACT.Copy, scale=vec(1, n))
@@ -230,7 +238,7 @@ def tile_list_ridge_region_scorer_kernel(
             x = ring.tile([P, R], BF16, name="x_tile", tag="x_tile", bufs=2)
             nc.vector.tensor_tensor(x[:], picked[0][:, t, :], picked[1][:, t, :], ALU.min)
             for j in range(PACK):
-                nc.sync.dma_start(x_rows[32 * t : 32 * t + 32, j, :], x[j:P:PACK, :])
+                nc.sync.dma_start(x_rows[QUADRANT * t : QUADRANT * (t + 1), j, :], x[j:P:PACK, :])
 
         def lesser_dealt():
             x = ring.tile([P, R, PACK], BF16, name="grouped", tag="grouped", bufs=4, align_bytes=64)
@@ -272,8 +280,8 @@ def tile_list_ridge_region_scorer_kernel(
             width = S // pieces
             for i in range(pieces):
                 cols = slice(i * width, (i + 1) * width)
-                lst = pos3_sb[:, i * width // 16 : (i + 1) * width // 16]
-                nc.vector.tensor_tensor(d[:, cols], win[:].indirect(lst), own[n][:, cols], ALU.add)
+                entries = pos3_sb[:, i * width // PER_COLUMN : (i + 1) * width // PER_COLUMN]
+                nc.vector.tensor_tensor(d[:, cols], win[:].indirect(entries), own[n][:, cols], ALU.add)
             for i in range(pieces):
                 cols = slice(i * width, (i + 1) * width)
                 nc.scalar.activation(d[:, cols], d[:, cols], ACT.Abs)
@@ -283,47 +291,50 @@ def tile_list_ridge_region_scorer_kernel(
                     nc.scalar.activation(d[:, cols], d[:, cols], ACT.Identity, bias=vec(2, n))
                 store(n, d, cols)
 
-        def stream_weight(slot, name, w, a, b):
-            raw = load_weight(head.tile([P, PACK, PASS], F32, name="raw_%s_%d_%d" % (name, a, b), offset=8192 * slot), w, a, b * PASS, name == "w2" and a == 1)
-            if b:
-                cast_dealt((name, a, b * PACK), raw)
+        def stream_weight(slot, name, w, a, dealt):
+            raw = head.tile([P, PACK, PASS], F32, name="raw_%s_%d_%d" % (name, a, dealt), offset=RAW_SLOT * slot)
+            load_weight(raw, w, a, dealt * PASS, name == "w2" and a == 1)
+            if dealt:
+                cast_dealt((name, a, PACK), raw)
             else:
                 cast_plain((name, a, 0), raw[:])
 
-        later = [("w1", w1, 0, 1), ("w1", w1, 1, 1), ("w2", w2, 0, 1), ("w2", w2, 1, 1), ("w2", w2, 0, 0), ("w2", w2, 1, 0)]
+        later = [("w1", w1, a, 1) for a in range(PASSES)]
+        later.extend([("w2", w2, a, dealt) for dealt in (1, 0) for a in range(PASSES)])
+        held_back = 2
         for n in range(TILES):
             for half in range(S // BANK):
-                product_a(n, half)
-                product_b(n, half)
+                product_w1(n, half)
+                product_w4(n, half)
             if n < 2:
                 c0, c1 = ((0, P), (P, rest))[n]
                 for a in range(PASSES):
                     cast_plain(("w1", a, n + 1), rest_raw[a][:, :, c0:c1])
-                    quantise(("w1", a, n + 1), n + 1)
-            if 2 <= n <= PACK + 1:
+                    quantise_weight(("w1", a, n + 1))
+            if 2 <= n < PACK + 2:
                 lesser_plain(n - 2)
             if n >= 1:
                 pick_pairs(n - 1)
                 scale_own(n - 1)
             if 1 <= n <= len(later):
                 stream_weight((n + 1) % 4, *later[n - 1])
-            if 2 <= n <= 5:
-                name, w, a, b = later[n - 2]
-                quantise((name, a, b * PACK), b * PACK)
-            if n == 6:
+            if 2 <= n < len(later) - held_back + 2:
+                name, w, a, dealt = later[n - 2]
+                quantise_weight((name, a, dealt * PACK))
+            if n == PACK + 2:
                 cast_plain(("x", 0, 0), x_rows[:])
-            if n == 7:
-                x_mx[0] = quantise(("x", 0, 0), 0)
+            if n == PACK + 3:
+                x_mx[0] = quantise(("x", 0, 0))
         pick_pairs(TILES - 1)
-        quantise(("w2", 0, 0), 0)
+        quantise_weight(("w2", 0, 0))
         lesser_dealt()
-        quantise(("w2", 1, 0), 0)
-        x_mx[1] = quantise(("x", 1, 0), 0)
+        quantise_weight(("w2", 1, 0))
+        x_mx[1] = quantise(("x", 1, 0))
         scale_own(TILES - 1)
-        order = [4, 5, 6, 7, 0, 1, 2, 3]
-        product_y(order[0], y_win[0])
-        product_y(order[1], y_win[1])
-        for i, n in enumerate(order):
+
+        for i in range(2):
+            product_y(SCORE_ORDER[i], y_win[i])
+        for i, n in enumerate(SCORE_ORDER):
             if i + 2 < TILES:
-                product_y(order[i + 2], y_win[(i + 2) % 3])
-            score(n, y_win[i % 3], 4 if i == TILES - 1 else 1)
+                product_y(SCORE_ORDER[i + 2], y_win[(i + 2) % 3])
+            score(n, y_win[i % 3], LAST_PIECES if i == TILES - 1 else 1)

from contextlib import ExitStack

import concourse.mybir as mybir
from concourse.masks import make_identity

K, H, T, S, R = 1024, 1024, 4096, 1024, 512
FLOPS = 2 * K * H * S * 2 + 2 * H * H * R

F32 = mybir.dt.float32
BF16 = mybir.dt.bfloat16
I32 = mybir.dt.int32
U32 = mybir.dt.uint32
U16 = mybir.dt.uint16
U8 = mybir.dt.uint8
FP8X4 = mybir.dt.float8_e4m3fn_x4
FP4X4 = mybir.dt.float4_e2m1fn_x4
ALU = mybir.AluOpType
ACT = mybir.ActivationFunctionType

P = 128
PACK = 4
PASS = P * PACK
PASSES = K // PASS
BANK = 512
TILES = H // P
PER_COLUMN = 16
QUADRANT = 32
Y_WINDOW = S + 16
RAW_SLOT = 4 * PACK * PASS
SCORE_ORDER = (4, 5, 6, 7, 0, 1, 2, 3)
LAST_PIECES = 4
BASE_ON_VECTOR = (3,)


def tile_list_ridge_region_scorer_kernel(
    tc, tab_words, tab_scales, offs, pos1, pos2, pos3, w1, w4_words, w4_scales, b4, w2, gain, base, out
):
    nc = tc.nc
    with ExitStack() as ctx:
        keep = ctx.enter_context(tc.tile_pool(name="keep", bufs=1))
        ring = ctx.enter_context(tc.tile_pool(name="ring", bufs=1))
        head = ctx.enter_context(tc.tile_pool(name="head", bufs=1))
        psum = ctx.enter_context(tc.psum_pool(name="psum", bufs=1))

        def load_list(name, src):
            t = keep.tile(list(src.shape), U16, name=name)
            nc.sync.dma_start(t[:], src)
            return t

        def load_scale_rows(t, src):
            nc.sync.dma_start(t[0:32, :].bitcast(I32), src.rearrange("a q c -> (a q) c").bitcast(I32))
            nc.vector.memset(t[32:64, :].bitcast(I32), 0)
            nc.vector.memset(t[64:P, :].bitcast(I32), 0)
            return t

        def load_table(t, a):
            nc.sync.dma_start(t[:], tab_words[a].rearrange("p t i -> p (t i)").bitcast(I32))
            return t

        def load_weight(raw, w, a, c0, dealt_rows=False):
            rows = w[a * PASS : (a + 1) * PASS, c0 : c0 + raw[:].shape[2]]
            if dealt_rows:
                for i in range(PACK):
                    nc.sync.dma_start(raw[i:P:PACK], rows.rearrange("(g j i) c -> i g j c", j=PACK, i=PACK)[i])
            else:
                nc.sync.dma_start(raw[:], rows.rearrange("(p j) c -> p j c", j=PACK))
            return raw

        ident = keep.tile([P, P], F32, name="ident")
        make_identity(nc, ident[:])
        vec_rows = keep.tile([P, PASS], F32, name="vec_rows")
        nc.vector.memset(vec_rows[:], 0.0)

        tab_s = load_scale_rows(keep.tile([P, T], U8, name="tab_s", align_bytes=64), tab_scales)
        offs_sb = load_list("offs_sb", offs)
        w4_s_raw = load_scale_rows(keep.tile([P, H], U8, name="w4_s_raw", align_bytes=64), w4_scales)
        w4_raw = keep.tile([P, PASSES, 2 * H], U8, name="w4_raw", align_bytes=64)
        nc.sync.dma_start(w4_raw[:].bitcast(I32), w4_words.rearrange("a p c -> p a c").bitcast(I32))
        pos1_sb = load_list("pos1_sb", pos1)
        pos2_sb = load_list("pos2_sb", pos2)
        pos3_sb = load_list("pos3_sb", pos3)
        tab = [load_table(keep.tile([P, T], I32, name="tab0", align_bytes=64), 0)]
        first_raw = [load_weight(keep.tile([P, PACK, P], F32, name="first%d" % a), w1, a, 0) for a in range(PASSES)]

        for i, src in enumerate((b4, gain, base)):
            nc.gpsimd.dma_start(vec_rows[2 * i : 2 * i + 2, :], src.rearrange("(b c) -> b c", b=2))
        vec_dealt = keep.tile([P, PASS], F32, name="vec_dealt")
        nc.scalar.activation(
            vec_dealt[:].rearrange("p (t g i) -> p t g i", t=PACK, i=PACK),
            vec_rows[:].rearrange("p (g t i) -> p t g i", t=PACK, i=PACK),
            ACT.Identity,
        )
        vecs = keep.tile([P, 2, PACK, 3], F32, name="vecs")
        for b in range(2):
            turned = psum.tile([P, PACK, P], F32, name="turned", tag="acc_y", bufs=2)
            for t in range(PACK):
                nc.tensor.transpose(turned[:, t, :], (vec_rows, vec_dealt)[b][:, t * P : (t + 1) * P], ident[:])
            nc.scalar.activation(vecs[:, b], turned[:, :, b:6:2], ACT.Identity)

        def vec(i, n):
            return vecs[:, n // PACK, n % PACK, i : i + 1]

        y_win = [keep.tile([P, Y_WINDOW], F32, name="y_win%d" % i, align_bytes=64) for i in range(3)]
        for t in y_win:
            nc.gpsimd.memset(t[:, R:], 0.0)

        planes = keep.tile([P, PASSES, S + H], U8, name="planes", align_bytes=64)
        nc.vector.memset(planes[:, 1, :].bitcast(I32), 0)
        picked_s = head.tile([P, 12 * S], U8, name="picked_s", offset=5 * S, align_bytes=64)[:, :S]
        nc.vector.tensor_copy(picked_s, tab_s[:].indirect(offs_sb[:]))
        nc.vector.tensor_copy(planes[:, 0, S : S + PASS].bitcast(I32), w4_s_raw[:, :PASS].bitcast(I32))
        nc.vector.tensor_copy(
            planes[:, 0, S + PASS :].bitcast(I32).rearrange("p (t g) -> p t g", t=PACK),
            w4_s_raw[:, PASS:].bitcast(I32).rearrange("p (g t) -> p t g", t=PACK),
        )
        nc.vector.tensor_copy(planes[:, 0, :S].bitcast(I32), picked_s.bitcast(I32))

        def move_scale_rows(a, q):
            row = 16 * a + 4 * q
            nc.sync.dma_start(
                planes[QUADRANT * q : QUADRANT * q + 4, a, :].bitcast(I32), planes[row : row + 4, 0, :].bitcast(I32)
            )

        for q in range(1, 4):
            move_scale_rows(0, q)
        tab.append(load_table(head.tile([P, T], I32, name="tab1", offset=2 * RAW_SLOT, align_bytes=64), 1))
        for q in range(4):
            move_scale_rows(1, q)
        rest = PASS - P
        rest_raw = [
            load_weight(head.tile([P, PACK, rest], F32, name="rest%d" % a, offset=4 * PACK * rest * a), w1, a, P)
            for a in range(PASSES)
        ]

        w4_dealt = keep.tile([P, PASSES, H], U8, name="w4_dealt", align_bytes=64)
        nc.vector.tensor_copy(
            w4_dealt[:].bitcast(I32).rearrange("p a (t g e) -> p a t g e", t=PACK, e=2),
            w4_raw[:, :, H:].bitcast(I32).rearrange("p a (g t e) -> p a t g e", t=PACK, e=2),
        )

        codes, scales, grouped = {}, {}, {}

        def cast_plain(key, raw_cols):
            width = raw_cols.shape[2]
            g = ring.tile([P, width, PACK], BF16, name="grouped", tag="grouped", bufs=4, align_bytes=64)
            nc.scalar.copy(
                g[:].rearrange("p (c i) j -> p c j i", i=4), raw_cols.rearrange("p j (c i) -> p c j i", i=4)
            )
            grouped[key] = g[:].rearrange("p m j -> p (m j)")

        def cast_dealt(key, raw):
            g = ring.tile([P, PACK, P, PACK], BF16, name="grouped", tag="grouped", bufs=4, align_bytes=64)
            nc.scalar.copy(
                g[:].rearrange("p t (g i) j -> p t g j i", i=PACK),
                raw[:].rearrange("p j (g t i) -> p t g j i", t=PACK, i=PACK),
            )
            grouped[key] = g[:].rearrange("p t m j -> p (t m j)")

        def quantise(key):
            src = grouped[key]
            width = src.shape[1] // PACK
            name = "%s_%d_%d" % key
            c = keep.tile([P, width], U32, name=name + "_q", align_bytes=64)
            s = keep.tile([P, width], U8, name=name + "_s", align_bytes=64)
            nc.vector.quantize_mx(out=c[:].bitcast(FP8X4), scales=s[:], in_=src)
            return c, s

        def quantise_weight(key):
            c, s = quantise(key)
            name, a, first_tile = key
            for i in range(c[:].shape[1] // P):
                codes[name, a, first_tile + i] = c[:, i * P : (i + 1) * P].bitcast(FP8X4)
                scales[name, a, first_tile + i] = s[:, i * P : (i + 1) * P]

        v_q = [keep.tile([P, S], U32, name="v_q%d" % a, align_bytes=64) for a in range(PASSES)]
        nc.vector.tensor_copy(v_q[0][:], tab[0][:].bitcast(U32).indirect(offs_sb[:]))
        for a in range(PASSES):
            cast_plain(("w1", a, 0), first_raw[a][:])
            quantise_weight(("w1", a, 0))
        for half in range(S // BANK):
            entries = offs_sb[:, half * BANK // PER_COLUMN : (half + 1) * BANK // PER_COLUMN]
            nc.vector.tensor_copy(v_q[1][:, half * BANK : (half + 1) * BANK], tab[1][:].bitcast(U32).indirect(entries))

        prod_w1, feats, own = {}, {}, {}

        def product_w1(n, half):
            if half == 0:
                prod_w1[n] = ring.tile([P, S], F32, name="a_sb", tag="a_sb", bufs=3)
            cols = slice(half * BANK, (half + 1) * BANK)
            acc = psum.tile([P, BANK], F32, name="acc_a", tag="acc_a", bufs=2)
            for a in range(PASSES):
                nc.tensor.matmul_mx(
                    out=acc[:],
                    lhsT=codes["w1", a, n],
                    lhsT_scale=scales["w1", a, n],
                    rhs=v_q[a][:, cols].bitcast(FP8X4),
                    rhs_scale=planes[:, a, cols],
                    start=(a == 0),
                    stop=(a == PASSES - 1),
                )
            nc.scalar.copy(prod_w1[n][:, cols], acc[:])

        def product_w4(n, half):
            dealt, t = divmod(n, PACK)
            if half == 0:
                feats[n] = ring.tile([P, S], F32, name="h", tag="row", bufs=5)
            cols = slice(half * BANK, (half + 1) * BANK)
            acc = psum.tile([P, BANK], F32, name="acc_b", tag="acc_b", bufs=4)
            words = w4_dealt if dealt else w4_raw
            for a in range(PASSES):
                nc.tensor.matmul_mx(
                    out=acc[:],
                    lhsT=words[:, a, 2 * P * t : 2 * P * (t + 1)].bitcast(FP4X4),
                    lhsT_scale=planes[:, a, S + P * n : S + P * (n + 1)],
                    rhs=v_q[a][:, cols].bitcast(FP8X4),
                    rhs_scale=planes[:, a, cols],
                    start=(a == 0),
                    stop=(a == PASSES - 1),
                )
            nc.vector.scalar_tensor_tensor(feats[n][:, cols], acc[:], vec(0, n), prod_w1[n][:, cols], ALU.add, ALU.mult)

        picked = [keep.tile([P, PACK, R], F32, name="pick%d" % i) for i in range(2)]
        x_rows = keep.tile([P, PACK, R], BF16, name="x_rows")

        def pick_pairs(n):
            t = n % PACK
            nc.vector.tensor_copy(picked[0][:, t, :], feats[n][:].indirect(pos1_sb[:]))
            nc.vector.tensor_copy(picked[1][:, t, :], feats[n][:].indirect(pos2_sb[:]))

        def scale_own(n):
            own[n] = keep.tile([P, S], F32, name="own%d" % n)
            if n == TILES - 1:
                nc.vector.tensor_scalar_mul(own[n][:], feats[n][:], vec(1, n))
            else:
                nc.scalar.activation(own[n][:], feats[n][:], ACT.Copy, scale=vec(1, n))

        def lesser_plain(t):
            x = ring.tile([P, R], BF16, name="x_tile", tag="x_tile", bufs=2)
            nc.vector.tensor_tensor(x[:], picked[0][:, t, :], picked[1][:, t, :], ALU.min)
            for j in range(PACK):
                nc.sync.dma_start(x_rows[QUADRANT * t : QUADRANT * (t + 1), j, :], x[j:P:PACK, :])

        def lesser_dealt():
            x = ring.tile([P, R, PACK], BF16, name="grouped", tag="grouped", bufs=4, align_bytes=64)
            nc.vector.tensor_tensor(
                x[:].rearrange("p (c i) t -> p c t i", i=2),
                picked[0][:].rearrange("p t (c i) -> p c t i", i=2),
                picked[1][:].rearrange("p t (c i) -> p c t i", i=2),
                ALU.min,
            )
            grouped["x", 1, 0] = x[:].rearrange("p m t -> p (m t)")

        out_dealt = out[PASS:, :].rearrange("(g t i) j -> t i g j", t=PACK, i=PACK)

        def store(n, d, cols):
            if n < PACK:
                nc.sync.dma_start(out[P * n : P * (n + 1), cols], d[:, cols])
            else:
                for i in range(PACK):
                    nc.sync.dma_start(out_dealt[n - PACK, i][:, cols], d[i:P:PACK, cols])

        x_mx = {}

        def product_y(n, win):
            acc = psum.tile([P, R], F32, name="acc_y", tag="acc_y", bufs=2)
            for a in range(PASSES):
                nc.tensor.matmul_mx(
                    out=acc[:],
                    lhsT=codes["w2", a, n],
                    lhsT_scale=scales["w2", a, n],
                    rhs=x_mx[a][0][:].bitcast(FP8X4),
                    rhs_scale=x_mx[a][1][:],
                    start=(a == 0),
                    stop=(a == PASSES - 1),
                )
            nc.scalar.activation(win[:, :R], acc[:], ACT.Copy, scale=-1.0)

        def score(n, win, pieces):
            d = ring.tile([P, S], F32, name="d", tag="row", bufs=5)
            width = S // pieces
            for i in range(pieces):
                cols = slice(i * width, (i + 1) * width)
                entries = pos3_sb[:, i * width // PER_COLUMN : (i + 1) * width // PER_COLUMN]
                nc.vector.tensor_tensor(d[:, cols], win[:].indirect(entries), own[n][:, cols], ALU.add)
            for i in range(pieces):
                cols = slice(i * width, (i + 1) * width)
                nc.scalar.activation(d[:, cols], d[:, cols], ACT.Abs)
                if n in BASE_ON_VECTOR:
                    nc.vector.tensor_scalar_add(d[:, cols], d[:, cols], vec(2, n))
                else:
                    nc.scalar.activation(d[:, cols], d[:, cols], ACT.Identity, bias=vec(2, n))
                store(n, d, cols)

        def stream_weight(slot, name, w, a, dealt):
            raw = head.tile([P, PACK, PASS], F32, name="raw_%s_%d_%d" % (name, a, dealt), offset=RAW_SLOT * slot)
            load_weight(raw, w, a, dealt * PASS, name == "w2" and a == 1)
            if dealt:
                cast_dealt((name, a, PACK), raw)
            else:
                cast_plain((name, a, 0), raw[:])

        later = [("w1", w1, a, 1) for a in range(PASSES)]
        later.extend([("w2", w2, a, dealt) for dealt in (1, 0) for a in range(PASSES)])
        held_back = 2
        for n in range(TILES):
            for half in range(S // BANK):
                product_w1(n, half)
                product_w4(n, half)
            if n < 2:
                c0, c1 = ((0, P), (P, rest))[n]
                for a in range(PASSES):
                    cast_plain(("w1", a, n + 1), rest_raw[a][:, :, c0:c1])
                    quantise_weight(("w1", a, n + 1))
            if 2 <= n < PACK + 2:
                lesser_plain(n - 2)
            if n >= 1:
                pick_pairs(n - 1)
                scale_own(n - 1)
            if 1 <= n <= len(later):
                stream_weight((n + 1) % 4, *later[n - 1])
            if 2 <= n < len(later) - held_back + 2:
                name, w, a, dealt = later[n - 2]
                quantise_weight((name, a, dealt * PACK))
            if n == PACK + 2:
                cast_plain(("x", 0, 0), x_rows[:])
            if n == PACK + 3:
                x_mx[0] = quantise(("x", 0, 0))
        pick_pairs(TILES - 1)
        quantise_weight(("w2", 0, 0))
        lesser_dealt()
        quantise_weight(("w2", 1, 0))
        x_mx[1] = quantise(("x", 1, 0))
        scale_own(TILES - 1)

        for i in range(2):
            product_y(SCORE_ORDER[i], y_win[i])
        for i, n in enumerate(SCORE_ORDER):
            if i + 2 < TILES:
                product_y(SCORE_ORDER[i + 2], y_win[(i + 2) % 3])
            score(n, y_win[i % 3], LAST_PIECES if i == TILES - 1 else 1)
